import numpy as np
import ml_dtypes


def mxq(x, axis, fmt="e4m3"):
    dtype, down = {"e4m3": (ml_dtypes.float8_e4m3fn, 7), "e5m2": (ml_dtypes.float8_e5m2, 14)}[fmt]
    v = np.moveaxis(np.asarray(x, np.float32).astype(ml_dtypes.bfloat16).astype(np.float64), axis, -1)
    blocks = v.reshape(v.shape[:-1] + (-1, 32))
    amax = np.abs(blocks).max(-1, keepdims=True)
    byte = np.maximum(np.where(amax > 0, np.frexp(amax)[1] - 1 + 127, 0) - down, 1)
    scale = np.exp2(byte - 127.0)
    codes = (blocks / scale).astype(np.float32).astype(dtype).astype(np.float64)
    return np.moveaxis((codes * scale).reshape(v.shape), -1, axis)


WIDE = False


def mx_kscale(k):
    if not WIDE:
        return np.ones(k)
    levels = np.array([10, -10, 5, -5, 0])
    if k % 512:
        return np.exp2(np.random.permutation(np.resize(levels, k // 32))).repeat(32)
    a = np.empty((k // 512, 16))
    for p in range(k // 512):
        a[p, :8] = np.random.permutation(np.resize(levels, 8))
        for g in range(8):
            far = levels[np.abs(levels - a[p, g]) >= 10]
            a[p, g + 8] = far[np.random.randint(len(far))]
    return np.exp2(a.ravel()).repeat(32)


def f64(x):
    return np.asarray(x).astype(np.float64)


def striped(idx):
    return np.tile(idx.reshape(-1, 16).T, (8, 1)).astype(np.uint16)


def unstriped(offs):
    return offs[:16].T.reshape(-1).astype(np.int64)


def pack_weight(w):
    k, n = w.shape
    w = f64(np.asarray(w, np.float32).astype(ml_dtypes.bfloat16)).reshape(k // 32, 32, n)
    amax = np.abs(w).max(1)
    byte = np.clip(np.where(amax > 0, np.frexp(amax)[1] - 1 + 127 - 7, 1), 1, 254)
    scaled = (w * np.exp2(127.0 - byte)[:, None, :]).reshape(k, n).astype(np.float32)
    words = np.ascontiguousarray(scaled.reshape(k // 512, 128, 4, n).transpose(0, 1, 3, 2)).astype(ml_dtypes.float8_e4m3fn).view(np.uint8)
    return words, np.ascontiguousarray(byte.astype(np.uint8).reshape(k // 512, 16, n))


def unpack_weight(words, scales):
    g, p, n, _ = words.shape
    vals = np.ascontiguousarray(words).view(ml_dtypes.float8_e4m3fn).astype(np.float64) * np.repeat(np.exp2(scales.astype(np.float64) - 127.0), 8, axis=1)[..., None]
    return vals.transpose(0, 1, 3, 2).reshape(g * 512, n)


K, T, E, C, N = 1024, 1024, 8, 256, 128


def by_expert(wq, xq):
    return np.concatenate([wq[e].T @ xq[:, e * C:(e + 1) * C] for e in range(E)], axis=1)


def setup_inputs():
    n = np.random.standard_normal
    s = mx_kscale(K)[:, None]
    first = np.random.permutation(np.repeat(np.arange(E), T // E))
    second = (first + 1 + np.random.permutation(np.repeat(np.arange(E - 1), -(-T // (E - 1)))[:T])) % E
    while np.bincount(second, minlength=E).max() != T // E:
        load = np.bincount(second, minlength=E); hi, lo = int(load.argmax()), int(load.argmin())
        t = np.flatnonzero((second == hi) & (first != lo))[0]; second[t] = lo
    slot_token = np.empty(E * C, np.int64); pos = np.empty((2, T), np.int64); fill = np.zeros(E, np.int64)
    place = np.stack([np.random.permutation(C) for _ in range(E)])
    for r, deal in enumerate((first, second)):
        for t in np.random.permutation(T):
            e = deal[t]; j = e * C + place[e, fill[e]]; fill[e] += 1; slot_token[j] = t; pos[r, t] = j
    g = np.random.uniform(0.2, 0.8, T)
    packed = [pack_weight(m) for m in n((E, K, N)) / np.sqrt(K) / s[None]]
    return {
        "xT": (n((K, T)) * s).astype(np.float32),
        "w_words": np.stack([m[0] for m in packed]),
        "w_scales": np.stack([m[1] for m in packed]),
        "gate": np.stack([np.tile(g, (N, 1)), np.tile(1.0 - g, (N, 1))]).astype(np.float32),
        "offs": striped(slot_token),
        "pos1": striped(pos[0]),
        "pos2": striped(pos[1]),
    }


def reference(xT, w_words, w_scales, gate, offs, pos1, pos2):
    idx = unstriped(offs)
    xq = mxq(f64(xT)[:, idx], 0, "e4m3")
    w = np.stack([unpack_weight(w_words[e], w_scales[e]) for e in range(E)])
    y = by_expert(w, xq)
    return f64(gate[0]) * y[:, unstriped(pos1)] + f64(gate[1]) * y[:, unstriped(pos2)]

@@ -1,0 +1,161 @@
+from contextlib import ExitStack
+
+import concourse.mybir as mybir
+
+K, T, E, C, N = 1024, 1024, 8, 256, 128
+FLOPS = 2 * K * N * E * C
+
+F32 = mybir.dt.float32
+BF16 = mybir.dt.bfloat16
+U32 = mybir.dt.uint32
+I32 = mybir.dt.int32
+U16 = mybir.dt.uint16
+U8 = mybir.dt.uint8
+FP8X4 = mybir.dt.float8_e4m3fn_x4
+MULT = mybir.AluOpType.mult
+ADD = mybir.AluOpType.add
+
+P = 128
+PACK = 4
+PASSES = K // (P * PACK)
+SLOTS = E * C
+TC = 256
+NCH = T // TC
+FAST = True
+
+WORD_CUTS_FIRST = (768, 768, 512)
+STEPS = (("b", 0, 3), ("w", 0, 3), ("b", 3, 3), ("w", 3, 3), ("b", 6, 2), ("w", 6, 1), ("w", 7, 1))
+OUT_CUTS = (256, 256, 256, 256)
+
+
+def spans(cuts):
+    res = []
+    lo = 0
+    for n in cuts:
+        res.append((lo, lo + n))
+        lo += n
+    return res
+
+
+def tile_routed_moe_kernel(tc, xT, w_words, w_scales, gate, offs, pos1, pos2, out):
+    nc = tc.nc
+    with ExitStack() as ctx:
+        held = ctx.enter_context(tc.tile_pool(name="held", bufs=1))
+        psum = ctx.enter_context(tc.psum_pool(name="psum", bufs=1))
+
+        offs_t = held.tile([P, SLOTS // 16], U16, name="offs_t")
+        pos1_t = held.tile([P, T // 16], U16, name="pos1_t")
+        pos2_t = held.tile([P, T // 16], U16, name="pos2_t")
+
+        tok_bytes = held.tile([P, T], U8, name="tok_bytes", align_bytes=64)
+        nc.gpsimd.memset(tok_bytes[:], 0)
+        w_planes = held.tile([P, E * N], U8, name="w_planes", align_bytes=64)
+        nc.vector.memset(w_planes[:].bitcast(I32), 0)
+        warm_in = held.tile([P, 8], F32, name="warm_in")
+        warm_out = held.tile([P, 8], F32, name="warm_out")
+        nc.vector.memset(warm_in[:], 0.0)
+        nc.scalar.copy(out=warm_out[:], in_=warm_in[:])
+
+        nc.sync.dma_start(offs_t[:], offs)
+        x_view = xT.rearrange("(a p j) t -> a p j t", p=P, j=PACK)
+        raw = {}
+        for a in range(PASSES):
+            for c in range(NCH):
+                raw[(a, c)] = held.tile([P, PACK, TC], F32, name="raw_%d_%d" % (a, c))
+                nc.sync.dma_start(out=raw[(a, c)][:], in_=x_view[a, :, :, c * TC:(c + 1) * TC])
+        w_codes = held.tile([P, E * PASSES, N], I32, name="w_codes", align_bytes=64)
+        nc.sync.dma_start(out=w_codes[:], in_=w_words.rearrange("e a p n r -> p (e a) (n r)").bitcast(I32))
+        for a in range(PASSES):
+            for q in range(4):
+                row = 32 * q + 4 * a
+                nc.sync.dma_start(
+                    out=w_planes[row:row + 4, :].bitcast(I32).rearrange("r (e n) -> r e n", e=E),
+                    in_=w_scales[:, a, 4 * q:4 * q + 4, :].bitcast(I32).rearrange("e r n -> r e n"),
+                )
+        gate_t = []
+        for r in range(2):
+            g = held.tile([P, T], F32, name="gate_%d" % r)
+            nc.sync.dma_start(out=g[:], in_=gate[r])
+            gate_t.append(g)
+        nc.sync.dma_start(pos1_t[:], pos1)
+        nc.sync.dma_start(pos2_t[:], pos2)
+
+        tok_words = [held.tile([P, T], U32, name="tok_words_%d" % a, align_bytes=64) for a in range(PASSES)]
+        grouped = [held.tile([P, T, PACK], BF16, name="grouped_%d" % a, align_bytes=64) for a in range(PASSES)]
+
+        def interleave(engine_copy, a, c):
+            dst = grouped[a][:, c * TC:(c + 1) * TC, :]
+            src = raw[(a, c)][:]
+            if FAST:
+                engine_copy(out=dst.rearrange("p (c i) j -> p c j i", i=4), in_=src.rearrange("p j (c i) -> p c j i", i=4))
+            else:
+                engine_copy(out=dst, in_=src.rearrange("p j t -> p t j"))
+
+        def quantise(a, lo, hi):
+            nc.vector.quantize_mx(
+                out=tok_words[a][:, lo:hi].bitcast(FP8X4),
+                scales=tok_bytes[4 * a:P, lo:hi],
+                in_=grouped[a][:, lo:hi, :].rearrange("p t j -> p (t j)"),
+            )
+
+        for c in range(NCH):
+            interleave(nc.scalar.copy if c % 2 == 0 else nc.vector.tensor_copy, 0, c)
+        for c in range(NCH):
+            quantise(0, c * TC, (c + 1) * TC)
+        for c in range(NCH):
+            interleave(nc.scalar.copy, 1, c)
+
+        got_words = [held.tile([P, SLOTS], U32, name="got_words_%d" % a, align_bytes=64) for a in range(PASSES)]
+        got_bytes = held.tile([P, SLOTS], U8, name="got_bytes", align_bytes=64)
+
+        def gather(dst, window, lo, hi):
+            nc.vector.tensor_copy(dst[:, lo:hi], window[:].indirect(offs_t[:, lo // 16:hi // 16]))
+
+        for lo, hi in spans(WORD_CUTS_FIRST):
+            gather(got_words[0], tok_words[0], lo, hi)
+        for h in range(2):
+            quantise(1, h * 512, (h + 1) * 512)
+
+        banks = [psum.tile([P, 512], F32, name="bank_%d" % e) for e in range(E)]
+        y_sb = held.tile([P, SLOTS], F32, name="y_sb")
+
+        def multiply(e, a):
+            nc.tensor.matmul_mx(
+                out=banks[e][:, 0:C],
+                lhsT=w_codes[:, e * PASSES + a, :].bitcast(FP8X4),
+                lhsT_scale=w_planes[4 * a:P, e * N:(e + 1) * N],
+                rhs=got_words[a][:, e * C:(e + 1) * C].bitcast(FP8X4),
+                rhs_scale=got_bytes[4 * a:P, e * C:(e + 1) * C],
+                start=(a == 0),
+                stop=(a == PASSES - 1),
+            )
+
+        for sort, e_lo, n_e in STEPS:
+            if sort == "b":
+                gather(got_bytes, tok_bytes, e_lo * C, (e_lo + n_e) * C)
+                for e in range(e_lo, e_lo + n_e):
+                    multiply(e, 0)
+            else:
+                gather(got_words[1], tok_words[1], e_lo * C, (e_lo + n_e) * C)
+                for e in range(e_lo, e_lo + n_e):
+                    multiply(e, 1)
+                    nc.scalar.copy(out=y_sb[:, e * C:(e + 1) * C], in_=banks[e][:, 0:C])
+
+        first = held.tile([P, T], F32, name="first")
+        second = held.tile([P, T], F32, name="second")
+        total = held.tile([P, T], F32, name="total")
+
+        def fetch(lo, hi):
+            nc.vector.tensor_tensor(first[:, lo:hi], y_sb[:].indirect(pos1_t[:, lo // 16:hi // 16]), gate_t[0][:, lo:hi], MULT)
+            nc.vector.tensor_tensor(second[:, lo:hi], y_sb[:].indirect(pos2_t[:, lo // 16:hi // 16]), gate_t[1][:, lo:hi], MULT)
+
+        def add_and_store(lo, hi):
+            nc.vector.tensor_tensor(total[:, lo:hi], first[:, lo:hi], second[:, lo:hi], ADD)
+            nc.sync.dma_start(out=out[:, lo:hi], in_=total[:, lo:hi])
+
+        out_spans = spans(OUT_CUTS)
+        fetch(*out_spans[0])
+        for i in range(1, len(out_spans)):
+            fetch(*out_spans[i])
+            add_and_store(*out_spans[i - 1])
+        add_and_store(*out_spans[-1])

@@ -1,6 +1,7 @@
 from contextlib import ExitStack
 
 import concourse.mybir as mybir
+from concourse.masks import make_identity
 
 K, T, E, C, N = 1024, 1024, 8, 256, 128
 FLOPS = 2 * K * N * E * C
@@ -25,7 +26,8 @@ FAST = True
 
 WORD_CUTS_FIRST = (768, 768, 512)
 STEPS = (("b", 0, 3), ("w", 0, 3), ("b", 3, 3), ("w", 3, 3), ("b", 6, 2), ("w", 6, 1), ("w", 7, 1))
-OUT_CUTS = (256, 256, 256, 256)
+OUT_CUTS = (256, 256, 256, 128, 128)
+ON_TENSOR = 2
 
 
 def spans(cuts):
@@ -55,6 +57,8 @@ def tile_routed_moe_kernel(tc, xT, w_words, w_scales, gate, offs, pos1, pos2, ou
         warm_out = held.tile([P, 8], F32, name="warm_out")
         nc.vector.memset(warm_in[:], 0.0)
         nc.scalar.copy(out=warm_out[:], in_=warm_in[:])
+        ident = held.tile([P, P], F32, name="ident")
+        make_identity(nc, ident[:])
 
         nc.sync.dma_start(offs_t[:], offs)
         x_view = xT.rearrange("(a p j) t -> a p j t", p=P, j=PACK)
@@ -141,21 +145,37 @@ def tile_routed_moe_kernel(tc, xT, w_words, w_scales, gate, offs, pos1, pos2, ou
                     multiply(e, 1)
                     nc.scalar.copy(out=y_sb[:, e * C:(e + 1) * C], in_=banks[e][:, 0:C])
 
-        first = held.tile([P, T], F32, name="first")
-        second = held.tile([P, T], F32, name="second")
-        total = held.tile([P, T], F32, name="total")
-
-        def fetch(lo, hi):
-            nc.vector.tensor_tensor(first[:, lo:hi], y_sb[:].indirect(pos1_t[:, lo // 16:hi // 16]), gate_t[0][:, lo:hi], MULT)
-            nc.vector.tensor_tensor(second[:, lo:hi], y_sb[:].indirect(pos2_t[:, lo // 16:hi // 16]), gate_t[1][:, lo:hi], MULT)
-
-        def add_and_store(lo, hi):
-            nc.vector.tensor_tensor(total[:, lo:hi], first[:, lo:hi], second[:, lo:hi], ADD)
-            nc.sync.dma_start(out=out[:, lo:hi], in_=total[:, lo:hi])
-
         out_spans = spans(OUT_CUTS)
-        fetch(*out_spans[0])
-        for i in range(1, len(out_spans)):
-            fetch(*out_spans[i])
-            add_and_store(*out_spans[i - 1])
-        add_and_store(*out_spans[-1])
+        first = [held.tile([P, n], F32, name="first_%d" % i) for i, n in enumerate(OUT_CUTS)]
+        second = [held.tile([P, n], F32, name="second_%d" % i) for i, n in enumerate(OUT_CUTS)]
+        total = [held.tile([P, n], F32, name="total_%d" % i) for i, n in enumerate(OUT_CUTS)]
+
+        def fetch(i):
+            lo, hi = out_spans[i]
+            nc.vector.tensor_tensor(first[i][:], y_sb[:].indirect(pos1_t[:, lo // 16:hi // 16]), gate_t[0][:, lo:hi], MULT)
+            nc.vector.tensor_tensor(second[i][:], y_sb[:].indirect(pos2_t[:, lo // 16:hi // 16]), gate_t[1][:, lo:hi], MULT)
+
+        def store(i):
+            lo, hi = out_spans[i]
+            nc.sync.dma_start(out=out[:, lo:hi], in_=total[i][:])
+
+        def add_on_tensor(i):
+            n = OUT_CUTS[i]
+            acc = psum.tile([P, 512], F32, name="bank_%d" % i)
+            nc.tensor.matmul(acc[:, 0:n], lhsT=ident[:], rhs=first[i][:], start=True, stop=False)
+            nc.tensor.matmul(acc[:, 0:n], lhsT=ident[:], rhs=second[i][:], start=False, stop=True)
+            nc.scalar.copy(out=total[i][:], in_=acc[:, 0:n])
+            store(i)
+
+        def add_on_vector(i):
+            nc.vector.tensor_tensor(total[i][:], first[i][:], second[i][:], ADD)
+            store(i)
+
+        for i in range(ON_TENSOR):
+            fetch(i)
+            add_on_tensor(i)
+        fetch(ON_TENSOR)
+        for i in range(ON_TENSOR + 1, len(OUT_CUTS)):
+            fetch(i)
+            add_on_vector(i - 1)
+        add_on_vector(len(OUT_CUTS) - 1)

@@ -20,9 +20,9 @@ P = 128
 PACK = 4
 PASSES = K // (P * PACK)
 SLOTS = E * C
-TC = 256
-NCH = T // TC
-FAST = True
+LOADS = ((512, 256, 256), (256, 256, 256, 256))
+VECTOR_SHARE = {512: 320, 256: 192}
+QUANTS = (LOADS[0], (512, 256, 256))
 
 WORD_CUTS_FIRST = (768, 768, 512)
 STEPS = (("b", 0, 3), ("w", 0, 3), ("b", 3, 3), ("w", 3, 3), ("b", 6, 2), ("w", 6, 1), ("w", 7, 1))
@@ -60,13 +60,14 @@ def tile_routed_moe_kernel(tc, xT, w_words, w_scales, gate, offs, pos1, pos2, ou
         ident = held.tile([P, P], F32, name="ident")
         make_identity(nc, ident[:])
 
-        nc.sync.dma_start(offs_t[:], offs)
         x_view = xT.rearrange("(a p j) t -> a p j t", p=P, j=PACK)
         raw = {}
         for a in range(PASSES):
-            for c in range(NCH):
-                raw[(a, c)] = held.tile([P, PACK, TC], F32, name="raw_%d_%d" % (a, c))
-                nc.sync.dma_start(out=raw[(a, c)][:], in_=x_view[a, :, :, c * TC:(c + 1) * TC])
+            for lo, hi in spans(LOADS[a]):
+                raw[(a, lo)] = held.tile([P, PACK, hi - lo], F32, name="raw_%d_%d" % (a, lo))
+                nc.sync.dma_start(out=raw[(a, lo)][:], in_=x_view[a, :, :, lo:hi])
+            if a == 0:
+                nc.sync.dma_start(offs_t[:], offs)
         w_codes = held.tile([P, E * PASSES, N], I32, name="w_codes", align_bytes=64)
         nc.sync.dma_start(out=w_codes[:], in_=w_words.rearrange("e a p n r -> p (e a) (n r)").bitcast(I32))
         for a in range(PASSES):
@@ -87,13 +88,10 @@ def tile_routed_moe_kernel(tc, xT, w_words, w_scales, gate, offs, pos1, pos2, ou
         tok_words = [held.tile([P, T], U32, name="tok_words_%d" % a, align_bytes=64) for a in range(PASSES)]
         grouped = [held.tile([P, T, PACK], BF16, name="grouped_%d" % a, align_bytes=64) for a in range(PASSES)]
 
-        def interleave(engine_copy, a, c):
-            dst = grouped[a][:, c * TC:(c + 1) * TC, :]
-            src = raw[(a, c)][:]
-            if FAST:
-                engine_copy(out=dst.rearrange("p (c i) j -> p c j i", i=4), in_=src.rearrange("p j (c i) -> p c j i", i=4))
-            else:
-                engine_copy(out=dst, in_=src.rearrange("p j t -> p t j"))
+        def interleave(engine_copy, a, base, lo, hi):
+            dst = grouped[a][:, lo:hi, :]
+            src = raw[(a, base)][:, :, lo - base:hi - base]
+            engine_copy(out=dst.rearrange("p (c i) j -> p c j i", i=4), in_=src.rearrange("p j (c i) -> p c j i", i=4))
 
         def quantise(a, lo, hi):
             nc.vector.quantize_mx(
@@ -102,12 +100,13 @@ def tile_routed_moe_kernel(tc, xT, w_words, w_scales, gate, offs, pos1, pos2, ou
                 in_=grouped[a][:, lo:hi, :].rearrange("p t j -> p (t j)"),
             )
 
-        for c in range(NCH):
-            interleave(nc.scalar.copy if c % 2 == 0 else nc.vector.tensor_copy, 0, c)
-        for c in range(NCH):
-            quantise(0, c * TC, (c + 1) * TC)
-        for c in range(NCH):
-            interleave(nc.scalar.copy, 1, c)
+        for lo, hi in spans(LOADS[0]):
+            cut = lo + VECTOR_SHARE[hi - lo]
+            interleave(nc.vector.tensor_copy, 0, lo, lo, cut)
+            interleave(nc.scalar.copy, 0, lo, cut, hi)
+            quantise(0, lo, hi)
+        for lo, hi in spans(LOADS[1]):
+            interleave(nc.scalar.copy, 1, lo, lo, hi)
 
         got_words = [held.tile([P, SLOTS], U32, name="got_words_%d" % a, align_bytes=64) for a in range(PASSES)]
         got_bytes = held.tile([P, SLOTS], U8, name="got_bytes", align_bytes=64)
@@ -117,8 +116,8 @@ def tile_routed_moe_kernel(tc, xT, w_words, w_scales, gate, offs, pos1, pos2, ou
 
         for lo, hi in spans(WORD_CUTS_FIRST):
             gather(got_words[0], tok_words[0], lo, hi)
-        for h in range(2):
-            quantise(1, h * 512, (h + 1) * 512)
+        for lo, hi in spans(QUANTS[1]):
+            quantise(1, lo, hi)
 
         banks = [psum.tile([P, 512], F32, name="bank_%d" % e) for e in range(E)]
         y_sb = held.tile([P, SLOTS], F32, name="y_sb")

@@ -21,8 +21,8 @@ PACK = 4
 PASSES = K // (P * PACK)
 SLOTS = E * C
 LOADS = ((512, 256, 256), (256, 256, 256, 256))
-VECTOR_SHARE = {512: 320, 256: 192}
-QUANTS = (LOADS[0], (512, 256, 256))
+COPIES = ((0, 0, 256, "s"), (0, 256, 512, "v"), (512, 512, 768, "s"), (768, 768, 1024, "v"))
+QUANTS = ((256, 256, 256, 256), (512, 512))
 
 WORD_CUTS_FIRST = (768, 768, 512)
 STEPS = (("b", 0, 3), ("w", 0, 3), ("b", 3, 3), ("w", 3, 3), ("b", 6, 2), ("w", 6, 1), ("w", 7, 1))
@@ -60,14 +60,13 @@ def tile_routed_moe_kernel(tc, xT, w_words, w_scales, gate, offs, pos1, pos2, ou
         ident = held.tile([P, P], F32, name="ident")
         make_identity(nc, ident[:])
 
+        nc.sync.dma_start(offs_t[:], offs)
         x_view = xT.rearrange("(a p j) t -> a p j t", p=P, j=PACK)
         raw = {}
         for a in range(PASSES):
             for lo, hi in spans(LOADS[a]):
                 raw[(a, lo)] = held.tile([P, PACK, hi - lo], F32, name="raw_%d_%d" % (a, lo))
                 nc.sync.dma_start(out=raw[(a, lo)][:], in_=x_view[a, :, :, lo:hi])
-            if a == 0:
-                nc.sync.dma_start(offs_t[:], offs)
         w_codes = held.tile([P, E * PASSES, N], I32, name="w_codes", align_bytes=64)
         nc.sync.dma_start(out=w_codes[:], in_=w_words.rearrange("e a p n r -> p (e a) (n r)").bitcast(I32))
         for a in range(PASSES):
@@ -100,10 +99,9 @@ def tile_routed_moe_kernel(tc, xT, w_words, w_scales, gate, offs, pos1, pos2, ou
                 in_=grouped[a][:, lo:hi, :].rearrange("p t j -> p (t j)"),
             )
 
-        for lo, hi in spans(LOADS[0]):
-            cut = lo + VECTOR_SHARE[hi - lo]
-            interleave(nc.vector.tensor_copy, 0, lo, lo, cut)
-            interleave(nc.scalar.copy, 0, lo, cut, hi)
+        for base, lo, hi, engine in COPIES:
+            interleave(nc.scalar.copy if engine == "s" else nc.vector.tensor_copy, 0, base, lo, hi)
+        for lo, hi in spans(QUANTS[0]):
             quantise(0, lo, hi)
         for lo, hi in spans(LOADS[1]):
             interleave(nc.scalar.copy, 1, lo, lo, hi)

@@ -68,7 +68,6 @@ def tile_routed_moe_kernel(tc, xT, w_words, w_scales, gate, offs, pos1, pos2, ou
                 raw[(a, lo)] = held.tile([P, PACK, hi - lo], F32, name="raw_%d_%d" % (a, lo))
                 nc.sync.dma_start(out=raw[(a, lo)][:], in_=x_view[a, :, :, lo:hi])
         w_codes = held.tile([P, E * PASSES, N], I32, name="w_codes", align_bytes=64)
-        nc.sync.dma_start(out=w_codes[:], in_=w_words.rearrange("e a p n r -> p (e a) (n r)").bitcast(I32))
         for a in range(PASSES):
             for q in range(4):
                 row = 32 * q + 4 * a
@@ -76,6 +75,8 @@ def tile_routed_moe_kernel(tc, xT, w_words, w_scales, gate, offs, pos1, pos2, ou
                     out=w_planes[row:row + 4, :].bitcast(I32).rearrange("r (e n) -> r e n", e=E),
                     in_=w_scales[:, a, 4 * q:4 * q + 4, :].bitcast(I32).rearrange("e r n -> r e n"),
                 )
+            if a == 0:
+                nc.sync.dma_start(out=w_codes[:], in_=w_words.rearrange("e a p n r -> p (e a) (n r)").bitcast(I32))
         gate_t = []
         for r in range(2):
             g = held.tile([P, T], F32, name="gate_%d" % r)

@@ -60,13 +60,14 @@ def tile_routed_moe_kernel(tc, xT, w_words, w_scales, gate, offs, pos1, pos2, ou
         ident = held.tile([P, P], F32, name="ident")
         make_identity(nc, ident[:])
 
-        nc.sync.dma_start(offs_t[:], offs)
         x_view = xT.rearrange("(a p j) t -> a p j t", p=P, j=PACK)
         raw = {}
         for a in range(PASSES):
             for lo, hi in spans(LOADS[a]):
                 raw[(a, lo)] = held.tile([P, PACK, hi - lo], F32, name="raw_%d_%d" % (a, lo))
                 nc.sync.dma_start(out=raw[(a, lo)][:], in_=x_view[a, :, :, lo:hi])
+            if a == 0:
+                nc.sync.dma_start(offs_t[:], offs)
         w_codes = held.tile([P, E * PASSES, N], I32, name="w_codes", align_bytes=64)
         for a in range(PASSES):
             for q in range(4):

@@ -25,7 +25,8 @@ COPIES = ((0, 0, 256, "s"), (0, 256, 512, "v"), (512, 512, 768, "s"), (768, 768,
 QUANTS = ((256, 256, 256, 256), (512, 512))
 
 WORD_CUTS_FIRST = (768, 768, 512)
-STEPS = (("b", 0, 3), ("w", 0, 3), ("b", 3, 3), ("w", 3, 3), ("b", 6, 2), ("w", 6, 1), ("w", 7, 1))
+GROUPS = (256, 256, 256, 256, 256, 256, 256, 128, 128)
+STEPS = (("b", 768), ("w", 768), ("b", 768), ("w", 768), ("b", 512), ("w", 256), ("w", 128), ("w", 128))
 OUT_CUTS = (256, 256, 256, 128, 128)
 ON_TENSOR = 2
 
@@ -119,30 +120,37 @@ def tile_routed_moe_kernel(tc, xT, w_words, w_scales, gate, offs, pos1, pos2, ou
         for lo, hi in spans(QUANTS[1]):
             quantise(1, lo, hi)
 
-        banks = [psum.tile([P, 512], F32, name="bank_%d" % e) for e in range(E)]
         y_sb = held.tile([P, SLOTS], F32, name="y_sb")
+        group_spans = spans(GROUPS)
+        banks = {}
 
-        def multiply(e, a):
+        def multiply(g, a):
+            lo, hi = group_spans[g]
+            e = lo // C
+            if a == 0:
+                banks[g] = psum.tile([P, 512], F32, name="bank_%d" % ((g + 2) % 8))
             nc.tensor.matmul_mx(
-                out=banks[e][:, 0:C],
+                out=banks[g][:, 0:hi - lo],
                 lhsT=w_codes[:, e * PASSES + a, :].bitcast(FP8X4),
                 lhsT_scale=w_planes[4 * a:P, e * N:(e + 1) * N],
-                rhs=got_words[a][:, e * C:(e + 1) * C].bitcast(FP8X4),
-                rhs_scale=got_bytes[4 * a:P, e * C:(e + 1) * C],
+                rhs=got_words[a][:, lo:hi].bitcast(FP8X4),
+                rhs_scale=got_bytes[4 * a:P, lo:hi],
                 start=(a == 0),
                 stop=(a == PASSES - 1),
             )
 
-        for sort, e_lo, n_e in STEPS:
-            if sort == "b":
-                gather(got_bytes, tok_bytes, e_lo * C, (e_lo + n_e) * C)
-                for e in range(e_lo, e_lo + n_e):
-                    multiply(e, 0)
-            else:
-                gather(got_words[1], tok_words[1], e_lo * C, (e_lo + n_e) * C)
-                for e in range(e_lo, e_lo + n_e):
-                    multiply(e, 1)
-                    nc.scalar.copy(out=y_sb[:, e * C:(e + 1) * C], in_=banks[e][:, 0:C])
+        done = {"b": 0, "w": 0}
+        for sort, n in STEPS:
+            lo, hi = done[sort], done[sort] + n
+            done[sort] = hi
+            gather(got_bytes if sort == "b" else got_words[1], tok_bytes if sort == "b" else tok_words[1], lo, hi)
+            for g, (g_lo, g_hi) in enumerate(group_spans):
+                if lo <= g_lo and g_hi <= hi:
+                    if sort == "b":
+                        multiply(g, 0)
+                    else:
+                        multiply(g, 1)
+                        nc.scalar.copy(out=y_sb[:, g_lo:g_hi], in_=banks[g][:, 0:g_hi - g_lo])
 
         out_spans = spans(OUT_CUTS)
         first = [held.tile([P, n], F32, name="first_%d" % i) for i, n in enumerate(OUT_CUTS)]

@@ -22,7 +22,7 @@ PASSES = K // (P * PACK)
 SLOTS = E * C
 LOADS = ((512, 256, 256), (256, 256, 256, 256))
 COPIES = ((0, 0, 256, "s"), (0, 256, 512, "v"), (512, 512, 768, "s"), (768, 768, 1024, "v"))
-QUANTS = ((256, 256, 256, 256), (512, 512))
+QUANTS = ((256, 256, 256, 256), (512, 256, 256))
 
 WORD_CUTS_FIRST = (768, 768, 512)
 GROUPS = (256, 256, 256, 256, 256, 256, 256, 128, 128)

@@ -21,7 +21,7 @@ PACK = 4
 PASSES = K // (P * PACK)
 SLOTS = E * C
 LOADS = ((512, 256, 256), (256, 256, 256, 256))
-COPIES = ((0, 0, 256, "s"), (0, 256, 512, "v"), (512, 512, 768, "s"), (768, 768, 1024, "v"))
+COPIES = ((0, 0, 256, "s"), (0, 256, 512, "v"), (512, 512, 768, "s"), (768, 768, 928, "v"), (768, 928, 1024, "s"))
 QUANTS = ((256, 256, 256, 256), (512, 256, 256))
 
 WORD_CUTS_FIRST = (768, 768, 512)

@@ -27,8 +27,8 @@ QUANTS = ((256, 256, 256, 256), (512, 256, 256))
 WORD_CUTS_FIRST = (768, 768, 512)
 GROUPS = (256, 256, 256, 256, 256, 256, 256, 128, 128)
 STEPS = (("b", 768), ("w", 768), ("b", 768), ("w", 768), ("b", 512), ("w", 256), ("w", 128), ("w", 128))
-OUT_CUTS = (256, 256, 256, 128, 128)
-ON_TENSOR = 2
+OUT_CUTS = (256, 256, 128, 256, 128)
+ON_TENSOR = 3
 
 
 def spans(cuts):
@@ -152,6 +152,9 @@ def tile_routed_moe_kernel(tc, xT, w_words, w_scales, gate, offs, pos1, pos2, ou
                         multiply(g, 1)
                         nc.scalar.copy(out=y_sb[:, g_lo:g_hi], in_=banks[g][:, 0:g_hi - g_lo])
 
+        warm = psum.tile([P, 512], F32, name="bank_7")
+        nc.tensor.matmul(warm[:, 0:256], lhsT=ident[:], rhs=y_sb[:, 1664:1920], start=True, stop=True)
+
         out_spans = spans(OUT_CUTS)
         first = [held.tile([P, n], F32, name="first_%d" % i) for i, n in enumerate(OUT_CUTS)]
         second = [held.tile([P, n], F32, name="second_%d" % i) for i, n in enumerate(OUT_CUTS)]
@@ -162,9 +165,9 @@ def tile_routed_moe_kernel(tc, xT, w_words, w_scales, gate, offs, pos1, pos2, ou
             nc.vector.tensor_tensor(first[i][:], y_sb[:].indirect(pos1_t[:, lo // 16:hi // 16]), gate_t[0][:, lo:hi], MULT)
             nc.vector.tensor_tensor(second[i][:], y_sb[:].indirect(pos2_t[:, lo // 16:hi // 16]), gate_t[1][:, lo:hi], MULT)
 
-        def store(i):
+        def store(queue, i):
             lo, hi = out_spans[i]
-            nc.sync.dma_start(out=out[:, lo:hi], in_=total[i][:])
+            queue.dma_start(out=out[:, lo:hi], in_=total[i][:])
 
         def add_on_tensor(i):
             n = OUT_CUTS[i]
@@ -172,11 +175,11 @@ def tile_routed_moe_kernel(tc, xT, w_words, w_scales, gate, offs, pos1, pos2, ou
             nc.tensor.matmul(acc[:, 0:n], lhsT=ident[:], rhs=first[i][:], start=True, stop=False)
             nc.tensor.matmul(acc[:, 0:n], lhsT=ident[:], rhs=second[i][:], start=False, stop=True)
             nc.scalar.copy(out=total[i][:], in_=acc[:, 0:n])
-            store(i)
+            store(nc.scalar, i)
 
         def add_on_vector(i):
             nc.vector.tensor_tensor(total[i][:], first[i][:], second[i][:], ADD)
-            store(i)
+            store(nc.sync, i)
 
         for i in range(ON_TENSOR):
             fetch(i)

@@ -27,8 +27,8 @@ QUANTS = ((256, 256, 256, 256), (512, 256, 256))
 WORD_CUTS_FIRST = (768, 768, 512)
 GROUPS = (256, 256, 256, 256, 256, 256, 256, 128, 128)
 STEPS = (("b", 768), ("w", 768), ("b", 768), ("w", 768), ("b", 512), ("w", 256), ("w", 128), ("w", 128))
-OUT_CUTS = (256, 256, 128, 256, 128)
-ON_TENSOR = 3
+OUT_CUTS = (320, 352, 192, 160)
+ON_TENSOR = 2
 
 
 def spans(cuts):

@@ -79,13 +79,10 @@ def tile_routed_moe_kernel(tc, xT, w_words, w_scales, gate, offs, pos1, pos2, ou
                 )
             if a == 0:
                 nc.sync.dma_start(out=w_codes[:], in_=w_words.rearrange("e a p n r -> p (e a) (n r)").bitcast(I32))
-        gate_t = []
-        for r in range(2):
-            g = held.tile([P, T], F32, name="gate_%d" % r)
-            nc.sync.dma_start(out=g[:], in_=gate[r])
-            gate_t.append(g)
         nc.sync.dma_start(pos1_t[:], pos1)
         nc.sync.dma_start(pos2_t[:], pos2)
+        gate_t = held.tile([P, 2, T], F32, name="gate_t")
+        nc.sync.dma_start(out=gate_t[:], in_=gate.rearrange("r p t -> p r t"))
 
         tok_words = [held.tile([P, T], U32, name="tok_words_%d" % a, align_bytes=64) for a in range(PASSES)]
         grouped = [held.tile([P, T, PACK], BF16, name="grouped_%d" % a, align_bytes=64) for a in range(PASSES)]
@@ -162,8 +159,8 @@ def tile_routed_moe_kernel(tc, xT, w_words, w_scales, gate, offs, pos1, pos2, ou
 
         def fetch(i):
             lo, hi = out_spans[i]
-            nc.vector.tensor_tensor(first[i][:], y_sb[:].indirect(pos1_t[:, lo // 16:hi // 16]), gate_t[0][:, lo:hi], MULT)
-            nc.vector.tensor_tensor(second[i][:], y_sb[:].indirect(pos2_t[:, lo // 16:hi // 16]), gate_t[1][:, lo:hi], MULT)
+            nc.vector.tensor_tensor(first[i][:], y_sb[:].indirect(pos1_t[:, lo // 16:hi // 16]), gate_t[:, 0, lo:hi], MULT)
+            nc.vector.tensor_tensor(second[i][:], y_sb[:].indirect(pos2_t[:, lo // 16:hi // 16]), gate_t[:, 1, lo:hi], MULT)
 
         def store(queue, i):
             lo, hi = out_spans[i]

from contextlib import ExitStack

import concourse.mybir as mybir
from concourse.masks import make_identity

K, T, E, C, N = 1024, 1024, 8, 256, 128
FLOPS = 2 * K * N * E * C

F32 = mybir.dt.float32
BF16 = mybir.dt.bfloat16
U32 = mybir.dt.uint32
I32 = mybir.dt.int32
U16 = mybir.dt.uint16
U8 = mybir.dt.uint8
FP8X4 = mybir.dt.float8_e4m3fn_x4
MULT = mybir.AluOpType.mult
ADD = mybir.AluOpType.add

P = 128
PACK = 4
PASSES = K // (P * PACK)
SLOTS = E * C
LOADS = ((512, 256, 256), (256, 256, 256, 256))
COPIES = ((0, 0, 256, "s"), (0, 256, 512, "v"), (512, 512, 768, "s"), (768, 768, 928, "v"), (768, 928, 1024, "s"))
QUANTS = ((256, 256, 256, 256), (512, 256, 256))

WORD_CUTS_FIRST = (768, 768, 512)
GROUPS = (256, 256, 256, 256, 256, 256, 256, 128, 128)
STEPS = (("b", 768), ("w", 768), ("b", 768), ("w", 768), ("b", 512), ("w", 256), ("w", 128), ("w", 128))
OUT_CUTS = (320, 352, 192, 160)
ON_TENSOR = 2


def spans(cuts):
    res = []
    lo = 0
    for n in cuts:
        res.append((lo, lo + n))
        lo += n
    return res


def tile_routed_moe_kernel(tc, xT, w_words, w_scales, gate, offs, pos1, pos2, out):
    nc = tc.nc
    with ExitStack() as ctx:
        held = ctx.enter_context(tc.tile_pool(name="held", bufs=1))
        psum = ctx.enter_context(tc.psum_pool(name="psum", bufs=1))

        offs_t = held.tile([P, SLOTS // 16], U16, name="offs_t")
        pos1_t = held.tile([P, T // 16], U16, name="pos1_t")
        pos2_t = held.tile([P, T // 16], U16, name="pos2_t")

        tok_bytes = held.tile([P, T], U8, name="tok_bytes", align_bytes=64)
        nc.gpsimd.memset(tok_bytes[:], 0)
        w_planes = held.tile([P, E * N], U8, name="w_planes", align_bytes=64)
        nc.vector.memset(w_planes[:].bitcast(I32), 0)
        warm_in = held.tile([P, 8], F32, name="warm_in")
        warm_out = held.tile([P, 8], F32, name="warm_out")
        nc.vector.memset(warm_in[:], 0.0)
        nc.scalar.copy(out=warm_out[:], in_=warm_in[:])
        ident = held.tile([P, P], F32, name="ident")
        make_identity(nc, ident[:])

        x_view = xT.rearrange("(a p j) t -> a p j t", p=P, j=PACK)
        raw = {}
        for a in range(PASSES):
            for lo, hi in spans(LOADS[a]):
                raw[(a, lo)] = held.tile([P, PACK, hi - lo], F32, name="raw_%d_%d" % (a, lo))
                nc.sync.dma_start(out=raw[(a, lo)][:], in_=x_view[a, :, :, lo:hi])
            if a == 0:
                nc.sync.dma_start(offs_t[:], offs)
        w_codes = held.tile([P, E * PASSES, N], I32, name="w_codes", align_bytes=64)
        for a in range(PASSES):
            for q in range(4):
                row = 32 * q + 4 * a
                nc.sync.dma_start(
                    out=w_planes[row:row + 4, :].bitcast(I32).rearrange("r (e n) -> r e n", e=E),
                    in_=w_scales[:, a, 4 * q:4 * q + 4, :].bitcast(I32).rearrange("e r n -> r e n"),
                )
            if a == 0:
                nc.sync.dma_start(out=w_codes[:], in_=w_words.rearrange("e a p n r -> p (e a) (n r)").bitcast(I32))
        nc.sync.dma_start(pos1_t[:], pos1)
        nc.sync.dma_start(pos2_t[:], pos2)
        gate_t = held.tile([P, 2, T], F32, name="gate_t")
        nc.sync.dma_start(out=gate_t[:], in_=gate.rearrange("r p t -> p r t"))

        tok_words = [held.tile([P, T], U32, name="tok_words_%d" % a, align_bytes=64) for a in range(PASSES)]
        grouped = [held.tile([P, T, PACK], BF16, name="grouped_%d" % a, align_bytes=64) for a in range(PASSES)]

        def interleave(engine_copy, a, base, lo, hi):
            dst = grouped[a][:, lo:hi, :]
            src = raw[(a, base)][:, :, lo - base:hi - base]
            engine_copy(out=dst.rearrange("p (c i) j -> p c j i", i=4), in_=src.rearrange("p j (c i) -> p c j i", i=4))

        def quantise(a, lo, hi):
            nc.vector.quantize_mx(
                out=tok_words[a][:, lo:hi].bitcast(FP8X4),
                scales=tok_bytes[4 * a:P, lo:hi],
                in_=grouped[a][:, lo:hi, :].rearrange("p t j -> p (t j)"),
            )

        for base, lo, hi, engine in COPIES:
            interleave(nc.scalar.copy if engine == "s" else nc.vector.tensor_copy, 0, base, lo, hi)
        for lo, hi in spans(QUANTS[0]):
            quantise(0, lo, hi)
        for lo, hi in spans(LOADS[1]):
            interleave(nc.scalar.copy, 1, lo, lo, hi)

        got_words = [held.tile([P, SLOTS], U32, name="got_words_%d" % a, align_bytes=64) for a in range(PASSES)]
        got_bytes = held.tile([P, SLOTS], U8, name="got_bytes", align_bytes=64)

        def gather(dst, window, lo, hi):
            nc.vector.tensor_copy(dst[:, lo:hi], window[:].indirect(offs_t[:, lo // 16:hi // 16]))

        for lo, hi in spans(WORD_CUTS_FIRST):
            gather(got_words[0], tok_words[0], lo, hi)
        for lo, hi in spans(QUANTS[1]):
            quantise(1, lo, hi)

        y_sb = held.tile([P, SLOTS], F32, name="y_sb")
        group_spans = spans(GROUPS)
        banks = {}

        def multiply(g, a):
            lo, hi = group_spans[g]
            e = lo // C
            if a == 0:
                banks[g] = psum.tile([P, 512], F32, name="bank_%d" % ((g + 2) % 8))
            nc.tensor.matmul_mx(
                out=banks[g][:, 0:hi - lo],
                lhsT=w_codes[:, e * PASSES + a, :].bitcast(FP8X4),
                lhsT_scale=w_planes[4 * a:P, e * N:(e + 1) * N],
                rhs=got_words[a][:, lo:hi].bitcast(FP8X4),
                rhs_scale=got_bytes[4 * a:P, lo:hi],
                start=(a == 0),
                stop=(a == PASSES - 1),
            )

        done = {"b": 0, "w": 0}
        for sort, n in STEPS:
            lo, hi = done[sort], done[sort] + n
            done[sort] = hi
            gather(got_bytes if sort == "b" else got_words[1], tok_bytes if sort == "b" else tok_words[1], lo, hi)
            for g, (g_lo, g_hi) in enumerate(group_spans):
                if lo <= g_lo and g_hi <= hi:
                    if sort == "b":
                        multiply(g, 0)
                    else:
                        multiply(g, 1)
                        nc.scalar.copy(out=y_sb[:, g_lo:g_hi], in_=banks[g][:, 0:g_hi - g_lo])

        warm = psum.tile([P, 512], F32, name="bank_7")
        nc.tensor.matmul(warm[:, 0:256], lhsT=ident[:], rhs=y_sb[:, 1664:1920], start=True, stop=True)

        out_spans = spans(OUT_CUTS)
        first = [held.tile([P, n], F32, name="first_%d" % i) for i, n in enumerate(OUT_CUTS)]
        second = [held.tile([P, n], F32, name="second_%d" % i) for i, n in enumerate(OUT_CUTS)]
        total = [held.tile([P, n], F32, name="total_%d" % i) for i, n in enumerate(OUT_CUTS)]

        def fetch(i):
            lo, hi = out_spans[i]
            nc.vector.tensor_tensor(first[i][:], y_sb[:].indirect(pos1_t[:, lo // 16:hi // 16]), gate_t[:, 0, lo:hi], MULT)
            nc.vector.tensor_tensor(second[i][:], y_sb[:].indirect(pos2_t[:, lo // 16:hi // 16]), gate_t[:, 1, lo:hi], MULT)

        def store(queue, i):
            lo, hi = out_spans[i]
            queue.dma_start(out=out[:, lo:hi], in_=total[i][:])

        def add_on_tensor(i):
            n = OUT_CUTS[i]
            acc = psum.tile([P, 512], F32, name="bank_%d" % i)
            nc.tensor.matmul(acc[:, 0:n], lhsT=ident[:], rhs=first[i][:], start=True, stop=False)
            nc.tensor.matmul(acc[:, 0:n], lhsT=ident[:], rhs=second[i][:], start=False, stop=True)
            nc.scalar.copy(out=total[i][:], in_=acc[:, 0:n])
            store(nc.scalar, i)

        def add_on_vector(i):
            nc.vector.tensor_tensor(total[i][:], first[i][:], second[i][:], ADD)
            store(nc.sync, i)

        for i in range(ON_TENSOR):
            fetch(i)
            add_on_tensor(i)
        fetch(ON_TENSOR)
        for i in range(ON_TENSOR + 1, len(OUT_CUTS)):
            fetch(i)
            add_on_vector(i - 1)
        add_on_vector(len(OUT_CUTS) - 1)
